import numpy as np, ml_dtypes
CORES = [242,247,114,119]
N = 4
BF = ml_dtypes.bfloat16
def gentries(a):
    return np.ascontiguousarray(a.reshape(8, 16, -1).transpose(0, 2, 1)).reshape(8, -1)
def gtable(e):
    e = np.asarray(e); return np.ascontiguousarray(e.reshape(8, -1, 16).transpose(0, 2, 1)).reshape(128, -1).astype(np.int32)
V, G, NB, RO, HP = 768, 384, 1, 5, 3
H = NB * G
S = V + H
def vals(rng, n):
    p = rng.choice(np.array([0.5, 1.0, 1.0, 2.0]), (N, 8, 1, n)) * rng.choice(np.array([0.7, 1.0, 1.4]), (N, 8, 16, 1))
    return np.minimum((256 * rng.random((N, 8, 16, n)) ** p).astype(np.int64), 255)
def parts(rng):
    m = rng.choice(np.array([2, 4, 16, 16]), (N, 8, 1, V))
    e = np.take_along_axis(rng.integers(0, S, (N, 8, 16, V)), (rng.random((N, 8, 16, V)) * m).astype(np.int64), axis=2)
    share = np.where(rng.random((N, 8, 1, V)) < 0.03125, 1.0, rng.choice(np.array([0.0, 0.0, 0.1, 0.3]), (N, 8, 1, V)))
    e = e + S * (rng.random((N, 8, 16, V)) < share)
    u = rng.integers(0, 16 * V, (N, 8, 16, V)); s = rng.integers(0, V // 4, (N, 8, H))
    h = rng.choice(np.array([200, 600, 1000, 1300, 1600]), (N, 8, RO)) + rng.integers(0, 200, (N, 8, RO))
    return e, u, vals(rng, V), vals(rng, V), vals(rng, S), s, h
def pack(e, u, x, b, y, s, h):
    flat = lambda a: np.ascontiguousarray(a.reshape(N, 128, a.shape[-1]))
    return {"ent": flat(e).astype(np.int32), "usr": flat(u).astype(np.int32), "xa": flat(x).astype(np.float32).astype(BF), "bn": flat(b).astype(np.float32).astype(BF),
            "yc": flat(y).astype(np.float32).astype(BF), "snd": np.stack([gtable(a) for a in s]), "th": np.ascontiguousarray(h).astype(np.int32)}
def setup_inputs(rng):
    return pack(*parts(rng))
def setup_inputs_spread(rng):
    e, u, x, b, y, s, h = parts(rng)
    def uneven(n):
        v = np.minimum((np.exp2(8 * rng.random((N, 8, 1, n))) * rng.random((N, 8, 16, n))).astype(np.int64), 255)
        return np.where(rng.random((N, 8, 1, n)) < 0.5, v, 255 - v)
    src = np.minimum((S * rng.random((N, 8, 16, V)) ** rng.choice(np.array([0.3, 1.0, 3.0]), (N, 8, 1, 1))).astype(np.int64), S - 1)
    e = src + S * (e >= S)
    w = np.minimum((V * rng.random((N, 8, 16, V)) ** rng.choice(np.array([0.5, 1.0, 2.0]), (N, 8, 1, 1))).astype(np.int64), V - 1)
    u = 16 * w + rng.integers(0, 16, (N, 8, 16, V))
    h = np.minimum(np.exp2(12 * rng.random((N, 8, RO))).astype(np.int64) - 1, 4080)
    return pack(e, u, uneven(V), uneven(V), uneven(S), s, h)
def setup_inputs_ends(rng):
    def two(n):
        mode = rng.integers(0, 3, (N, 8, 1, n)); bits = rng.integers(0, 2, (N, 8, 16, n))
        return 255 * np.where(mode == 0, 0, np.where(mode == 1, 1, bits))
    def mix(top, share, other):
        return np.where(rng.random((N, 8, 16, V)) < share, top * rng.integers(0, 2, (N, 8, 16, V)), other)
    x, b, y = two(V), two(V), two(S); v = np.arange(V)
    near = rng.choice(np.array([0, V - 1, V, S - 1, S, S + V - 1, S + V]), (N, 8, 16, V))
    e = mix(2 * S - 1, 0.75, np.where(rng.random((N, 8, 16, V)) < 0.5, near, rng.integers(0, 2 * S, (N, 8, 16, V))))
    u = mix(16 * V - 1, 0.75, rng.integers(0, 16 * V, (N, 8, 16, V)))
    none = v % 8 == 2; one = rng.integers(0, 16, (N, 8, 1, V))
    e = np.where(none, 2 * S - 1, np.where(np.arange(16)[:, None] == one, 0, e))
    top = np.where(np.arange(8) % 2 == 0, 255, 0)[None, :, None]
    x[:, :, :, 0] = top; y[:, :, :, 0] = top; b[:, :, :, 0] = 0; e[:, :, :, 0] = 0
    u[:, :4, 0, 0] = 0; u[:, 4:, 0, 0] = 16 * V - 1
    far = list(range(1, 8)) + list(range(V - 8, V))
    x[:, :, :, far] = 255 - top[..., None]; b[:, :, :, far] = 0; e[:, :, :, far] = 0; u[:, :, 0, far] = 16 * V - 1
    lone = list(range(12, 16)) + list(range(V - 12, V - 8))
    x[:, :, :, lone] = 255 - top[..., None]; e[:, :, :15, lone] = 2 * S - 1; e[:, :, 15, lone] = 0
    still = list(range(8, 12))
    x[:, :, :, still] = top[..., None]; b[:, :, :, still] = 0; e[:, :, :, still] = 0; u[:, :, 0, still] = 0
    s = (V // 4 - 1) * rng.integers(0, 2, (N, 8, H))
    h = 4080 * rng.integers(0, 2, (N, 8, RO)); h[:, 0, 0] = 0; h[:, 1, 0] = 0; h[:, 6, 0] = 4080; h[:, 7, 0] = 4080; h[N - 1, :, 1] = 4080
    return pack(e, u, x, b, y, s, h)
def setup_inputs_corners(rng):
    e, u, x, b, y, s, h = parts(rng); v = np.arange(V)
    src = rng.integers(0, S, (N, 8, 16, V)); src[:, 3] = v; src[:, 5] = rng.integers(V, S, (N, 16, V))
    src[:, 6] = rng.choice(np.array([0, V - 1, V, S - 1]), (N, 16, V))
    cl = rng.choice(np.array([0, 1, 2, 15, 16]), (N, 8, 1, V)); cl[:, 5] = 16
    o = np.argsort(rng.random((N, 8, 16, V)), axis=2); o[:, 0] = np.arange(15, -1, -1)[:, None]; o[:, 7] = np.arange(16)[:, None]
    gone = o >= cl; gone[:, 4, 15] = True
    q = rng.integers(0, 16, (N, 8, 16, V))
    u[:, 1] = 16 * np.where(v < V // 2, v, v ^ 1) + q[:, 1]; u[:, 2] = 16 * ((v + 1) % V) + q[:, 2]
    u[:, 3] = 16 * rng.choice(np.array([0, V - 1]), (N, 16, V)) + q[:, 3]; u[:, 4] = 16 * (u[:, 4] >> 4) + 15
    e = src + S * gone
    for a in range(N):
        turn = np.roll(np.arange(8), a); e[a] = e[a][turn]; u[a] = u[a][turn]
    e[1, :, :, 2::4] = e[1, :, :, 2::4] % S + S
    s[:, ::2] = rng.choice(np.array([0, V // 4 - 1]), (N, 4, H))
    h = rng.choice(np.array([0, 1, 300, 1000, 1400, 4079, 4080]), (N, 8, RO))
    return pack(e, u, x, b, y, s, h)
def setup_inputs_limits(rng):
    e, u, x, b, y, s, h = parts(rng); m = V // 4; a = np.arange(N)[:, None]; g = np.arange(8)[None, :]; k = np.arange(16)[:, None]; p = rng.permutation(N)
    base = np.where((a + g) % 2 == 0, rng.integers(2048, 3824, (N, 8)), rng.integers(64, 1700, (N, 8)))
    eff = base[..., None] + np.argsort(rng.random((N, 8, m)), axis=2)
    d = (eff[:, :, None] + np.argsort(rng.random((N, 8, 16, m)), axis=2)) // 16
    mv = (rng.random((N, 8, 8, m)) * (np.minimum(255 - d[:, :, :8], d[:, :, 8:]) + 1)).astype(np.int64)
    d = np.concatenate([d[:, :, :8] + mv, d[:, :, 8:] - mv], axis=2)
    fv = (rng.random(d.shape) * (np.minimum(128, 255 - d) + 1)).astype(np.int64)
    x[..., 3::4] = np.where((fv >= d) & (rng.random(d.shape) < 0.5), fv - d, fv + d)
    b[..., 3::4] = np.where((fv < 128) & (rng.random(d.shape) < 0.5), 127 - fv, 127 + fv)
    w = 4 * np.argsort(rng.random((N, 8, 4, m)), axis=3) + 3
    u = 16 * w.transpose(0, 1, 3, 2).reshape(N, 8, 1, V) + rng.integers(8, 16, (N, 8, 16, V))
    e = np.where(k == rng.integers(0, 16, (N, 8, 1, V)), e % S, e)
    o = np.argsort(rng.random((N, 8, S)), axis=2); lo, hi = o[..., 0], o[..., 1]
    y[a, g, :, lo] = 0; y[a, g, :, hi] = 255; lo = lo[..., None]; hi = hi[..., None]
    c = rng.integers(0, 2, (N, 8, m)) == 1
    e[..., 3::4] = e[..., 3::4] % S + S * (k < 8)
    e[:, :, 0, 3::4] = S + np.where(c, lo, hi); e[:, :, 7, 3::4] = S + np.where(c, hi, lo)
    h = base[..., None] + rng.integers(32, m - 64, (N, 8, RO))
    h = h - (h & 15) + rng.choice(np.array([0, 1, 2, 3, 4, 5, 10, 11, 12, 13, 14, 15]), h.shape)
    h[p[:2], :, 0] = 4080; h[p[2:], rng.integers(0, 8, N - 2), 0] = 4080; h[p[1], :, 1] = 0
    few = 4 * rng.permutation(m)[:int(rng.integers(1, 32))]; ez = e[p[1], int(rng.integers(0, 8))]
    ez[:, few] = ez[:, few] % S + S
    e[p[1], ::2, :, 1::4] = e[p[1], ::2, :, 1::4] % S + S
    return pack(e, u, x, b, y, s, h)
def setup_inputs_ties(rng):
    e, u, x, b, y, s, h = parts(rng)
    base = rng.choice(np.array([0, 100, 252]), (N, 8, 1, 1)); base[:, 0] = 252; base[:, 7] = 0
    x = base + rng.integers(0, 4, (N, 8, 16, V)); y = base + rng.integers(0, 4, (N, 8, 16, S)); b = rng.integers(0, 4, (N, 8, 16, V))
    x[:, :, :, 1::4] = x[:, :, :, 0::4]; x[:, :, :, 3::4] = x[:, :, :, 2::4]
    h = rng.integers(0, 40, (N, 8, RO))
    return pack(e, u, x, b, y, s, h)
def check_inputs(d):
    bad = []
    for k, lo, hi in (("ent", 0, 2 * S - 1), ("usr", 0, 16 * V - 1), ("xa", 0, 255), ("bn", 0, 255), ("yc", 0, 255), ("snd", 0, V // 4 - 1), ("th", 0, 4080)):
        v = np.asarray(d[k]).astype(np.float64)
        if not np.all((v >= lo) & (v <= hi)): bad.append("range of " + k)
        elif np.any(v != np.floor(v)): bad.append("whole numbers of " + k)
    return bad
def mid(a, b):
    return np.abs(((np.maximum.reduce(a, axis=3) + np.minimum.reduce(a, axis=3)) >> 1) - b)
def nodes(a, dtype):
    return np.ascontiguousarray(np.asarray(a).astype(np.float32).astype(dtype).reshape(N, 8, 16, -1).transpose(0, 1, 3, 2))
def reference(ent, usr, xa, bn, yc, snd, th):
    e, u = nodes(ent, np.int64), nodes(usr, np.int64); x, b, y = nodes(xa, np.int32), nodes(bn, np.int32), nodes(yc, np.int32)
    sl = np.stack([gentries(a) for a in snd]).astype(np.int64).reshape(N, 8, NB, 4, G // 4) * 4 + np.arange(4)[:, None]
    sl = sl.reshape(N, 8, NB, G); hh = th.astype(np.int64)
    r3 = np.arange(N)[:, None, None]; g3 = np.arange(8)[None, :, None]; r4 = r3[..., None]; g4 = g3[..., None]; sixteen = np.arange(16)
    gone = np.zeros(N, np.int64)
    for t in range(RO):
        w = [x]
        for n in range(1, NB + 1):
            q = (np.arange(N) + n) % N
            w.append(x[q][r3, g3, sl[q, :, n - 1]])
        w = np.concatenate(w + [y], axis=2)
        own = np.arange(t % 4, V, 4)
        eo = e[:, :, own]; xo = x[:, :, own]; bo = b[:, :, own]
        src = w[r4, g4, eo]
        score = np.add.reduce(np.abs(src - xo[:, :, :, None]), axis=4); clean = eo < S; some = np.any(clean, axis=3)
        k = np.argmin(np.where(clean, score, 9999), axis=3)
        hit = (sixteen == k[..., None]) & some[..., None]
        ek = np.take_along_axis(eo, k[..., None], 3)[..., 0]
        cv = w[r3, g3, np.where(some, ek + S, 0)]
        f0 = mid(src, bo); z = mid(np.where(hit[..., None], cv[:, :, :, None], src), bo); z0 = z
        c = np.broadcast_to(own, some.shape); dead = np.zeros(some.shape, bool)
        for hop in range(HP):
            p = u[r3, g3, c, np.add.reduce(z, axis=3) & 15]
            c = p >> 4; at = sixteen == (p & 15)[..., None]; ew = e[r3, g3, c]
            dead = dead | np.any(at & (ew >= S), axis=3)
            z = mid(np.where(at[..., None], z[:, :, :, None], w[r4, g4, ew]), b[r3, g3, c])
        D = np.where(dead, 0, np.add.reduce(np.abs(z - x[r3, g3, c]), axis=3))
        stay = some & (D <= hh[:, :, t][..., None] + (gone & 31)[:, None, None])
        e[:, :, own] = np.where(stay[..., None] & hit, eo + S, eo)
        x[:, :, own] = np.where(stay[..., None], z0, f0)
        gone = np.add.reduce(stay.astype(np.int64), axis=(1, 2))
    return {"ye": np.ascontiguousarray(e.transpose(0, 1, 3, 2)).reshape(N, 128, V).astype(np.float32), "yx": np.ascontiguousarray(x.transpose(0, 1, 3, 2)).reshape(N, 128, V).astype(np.float32).astype(BF)}

import numpy as np
from concourse.mybir import AluOpType as OP, ActivationFunctionType as AF, AxisListType as AX

V, NG, NBT, PARTS = 768, 384, 96, 2
ZC = 288
XO = ZC
XG = ZC + V
YO = XG + NG
XE = ZC + 2304
MAGIC = 12582912.0
BF2 = "bfloat16"
SCRATCH = {}
WHERE = {}


def _buf(name, cols, dtype=BF2, where="sbuf", rows=128, pool=True):
    if not pool or where != "sbuf" or rows != 128 or cols > 144:
        SCRATCH[name] = (where, [rows, cols], dtype)
        WHERE[name] = (name, 0, cols, dtype)
        return
    p = "pool_" + dtype
    lo = SCRATCH[p][1][1] if p in SCRATCH else 0
    SCRATCH[p] = ("sbuf", [128, lo + (cols + 15) // 16 * 16], dtype)
    WHERE[name] = (p, lo, cols, dtype)


for _b in range(2):
    _buf("xw%d" % _b, XE)
    for _n in ("ga", "gb", "mt", "mx", "mn", "m0", "n0"):
        _buf("%s%d" % (_n, _b), 16 * NBT)
    for _n in ("f0", "hit", "pq", "bw", "xv", "z3", "da", "st", "sd", "hs", "da1", "da2", "da3"):
        _buf("%s%d" % (_n, _b), NBT)
    _buf("pw%d" % _b, NBT, "float16")
    for _n in ("hot", "aa", "ll", "of", "kt", "r1", "mb", "mbt"):
        _buf("%s%d" % (_n, _b), NBT, "float32")
    _buf("rm%d" % _b, 112, "float32")
    _buf("ri%d" % _b, NBT)
    _buf("ou%d" % _b, NBT, "uint16")
    _buf("eu%d" % _b, NBT, "uint16")
    _buf("wl%d" % _b, 8, "uint16")
for _n in ("enti", "usri", "uw", "uq"):
    _buf(_n, V, "int32")
_buf("entt", V, "float32")
_buf("yef", V, "float32")
_buf("ct", V)
_buf("bt", V)
_buf("sndi", 24, "int32", "sbuf", 128, False)
_buf("sndu", 24, "uint16")
_buf("thi", 5, "int32", "sbuf", 8)
_buf("thf", 5, "float32", "sbuf", 8)
for _n, _w in (("tha", 5), ("thc", 5), ("rr", 1), ("pf", 4), ("bc", 4), ("py", 1), ("mgc", 1), ("nzc", 1),
               ("rg", NBT), ("idf", 128)):
    _buf(_n, _w, "float32")
for _n, _w in (("rri", 1), ("rrj", 1), ("ji", NBT), ("jj", NBT), ("pi", 4), ("pj", 4), ("bi", 4)):
    _buf(_n, _w, "int32")
_buf("gs0", NG)
for _n in range(4):
    _buf("gt%d" % _n, NBT, BF2, "sbuf", 128, False)
    _buf("land%d" % _n, NBT, BF2, "sbuf", 128, False)
for _n in ("one", "idn", "half", "neg", "i256", "i1152", "b16", "b1", "b4096", "dead"):
    _buf(_n, 128)
for _n in ("one144", "blkh", "blk", "wsel", "w32", "w16", "wn16"):
    _buf(_n, 144)
_buf("blkf", 128, "float16")
for _n in ("oe", "ee0", "ee"):
    _buf(_n, 128, "float32", "sbuf", 8)
for _n in ("kc", "yc96", "jc", "mask", "cm", "cq"):
    _buf(_n, NBT)
_buf("ab1", 16 * NBT)
_buf("rx", 16 * NBT)
_buf("rn", 16 * NBT)
for _n in range(8):
    _buf("p%d" % _n, 512, "float32", "psum")
LOADS = ["snd", "xa", "ent", "yc", "bn", "usr", "th"]
SEMAPHORES = ["sv", "ss", "st", "sg", "loc", "o0", "o1", "o2", "o3"] + ["ld_" + n for n in LOADS] + ["arr%d" % t for t in range(5)]
QS = {"v": "sv", "s": "ss", "t": "st", "g": "sg"}
PLAN = {}


def _overlap(a, b):
    if a[1] >= b[2] or b[1] >= a[2]:
        return False
    return not (a[3] > 1 and a[3] == b[3] and (a[1] - b[1]) % a[3])


def _bank(r):
    return r[0][0] == "p" and r[0][1:].isdigit()


def _edges(ops):
    hist = {}
    for i, o in enumerate(ops):
        pre = {}
        both = [(False, r) for r in o["rd"]] + [(True, r) for r in o["wr"]]
        for wr, r in both:
            for (r2, j, w2) in hist.get(r[0], ()):
                if j == i or not (_bank(r) or ((wr or w2) and _overlap(r, r2))):
                    continue
                pre[j] = pre.get(j, False) or ops[j]["q"] != o["q"] or (w2 and (not wr or o["q"] != "t")) or ops[j]["dma"]
        for j in o["after"]:
            pre[j] = True
        for wr, r in both:
            h = hist.setdefault(r[0], [])
            if _bank(r):
                if h and ops[h[-1][1]]["q"] != o["q"]:
                    h[:] = [e for e in h if e[1] == i or ops[e[1]]["q"] != o["q"]]
            elif wr:
                h[:] = [e for e in h if e[1] == i or not (r == e[0] or (r[3] == 1 and r[1] <= e[0][1] and e[0][2] <= r[2]))]
            h.append((r, i, wr))
        o["pre"] = pre


def _cost(o, m):
    f, n, gath = o["cost"]
    return f * m[0] + max(64, n * (m[2] if gath else 1)) * 1.0e-3 * m[1] if n else f


def _schedule(ops, succ, m, slack, noise):
    n = len(ops)
    cost = [_cost(o, m) for o in ops]
    pri = [0.0] * n
    for i in range(n - 1, -1, -1):
        x = 0.0
        for j in succ[i]:
            x = max(x, pri[j] + (m[3] if ops[j]["pre"][i] else 0.0))
        pri[i] = x + cost[i] + ops[i]["lag"] * m[4]
    pri = [pri[i] + float(noise[i]) for i in range(n)]
    left = [len(o["pre"]) for o in ops]
    rdy = [0.0] * n
    cand = {}
    for i in range(n):
        if left[i] == 0:
            cand.setdefault(ops[i]["q"], []).append(i)
    free = {}
    order = []
    while True:
        q = None
        for k in cand:
            if cand[k]:
                s = max(free.get(k, 0.0), min(rdy[i] for i in cand[k]))
                if q is None or s < s0:
                    q, s0 = k, s
        if q is None:
            return order
        pick = None
        for i in cand[q]:
            if rdy[i] <= s0 + slack and (pick is None or pri[i] > pri[pick]):
                pick = i
        cand[q].remove(pick)
        order.append(pick)
        st = max(s0, rdy[pick])
        free[q] = st + cost[pick]
        for j in succ[pick]:
            e = free[q] + ops[pick]["lag"] * m[4] + m[3] if ops[j]["pre"][pick] else st
            rdy[j] = max(rdy[j], e)
            left[j] -= 1
            if left[j] == 0:
                cand.setdefault(ops[j]["q"], []).append(j)


def _length(ops, order, m):
    free, fin, top = {}, [0.0] * len(ops), 0.0
    for i in order:
        o = ops[i]
        t = free.get(o["q"], 0.0)
        for j in o["pre"]:
            if o["pre"][j]:
                t = max(t, fin[j] + m[3])
        free[o["q"]] = t + _cost(o, m)
        fin[i] = free[o["q"]] + o["lag"] * m[4]
        top = max(top, fin[i])
    return top


MODELS = [(1.0, 1.04, 1.56, 0.06, 1.0), (0.4, 0.9, 1.2, 0.06, 1.0), (0.5, 1.2, 2.0, 0.1, 1.3), (1.0, 0.9, 1.3, 0.2, 1.3)]
STEPS = 1600


def _plan(ops):
    succ = [[] for _ in ops]
    for i, o in enumerate(ops):
        for j in o["pre"]:
            succ[j].append(i)
    keys = 1 + max(o["key"] for o in ops)
    rng = np.random.RandomState(5)
    cur = np.full(keys + 1, 2.0)
    cur[keys] = 0.0
    best = None
    for step in range(STEPS):
        c = cur.copy()
        if step:
            if rng.rand() < 0.5:
                for _i in range((1, 2, 4, 10, 25)[rng.randint(5)]):
                    c[rng.randint(keys)] = 0.25 * rng.randint(26)
            else:
                a, w = rng.randint(keys), (3, 8, 20, 60)[rng.randint(4)]
                hi = min(keys, a + w)
                c[a:hi] = np.clip(c[a:hi] + 0.25 * rng.randint(-6, 7), 0.0, 6.25)
        order = _schedule(ops, succ, MODELS[0], 0.12, [float(c[o["key"]]) for o in ops])
        score = []
        for m in range(len(MODELS)):
            score.append(_length(ops, order, MODELS[m]))
            if best and m == 0 and score[0] > 1.006 * best[1][0]:
                break
        if len(score) < len(MODELS):
            continue
        if not best:
            base = score
        x = sum(a / b for a, b in zip(score, base))
        if not best or x <= best[0]:
            best, cur = (x, score, order), c
    return best[2]


def rank_program(g, core, T, topo):
    rank = T.rank_of(core)
    if rank is None:
        return
    ops = []
    start = []
    eng = {"v": g.vector, "s": g.scalar, "t": g.tensor, "g": g, "y": g.sync}

    def add(q, fn, rd, wr, cost, lag=0.0, sem=None, amount=1, dma=False, after=()):
        ops.append({"q": q, "fn": fn, "key": len(ops) - start[0] if start else -1, "rd": rd, "wr": wr, "cost": cost, "lag": lag, "sem": sem, "amount": amount,
                    "dma": dma, "after": list(after), "remote": False})
        return len(ops) - 1

    def A(name, lo=0, hi=None, step=1):
        buf, o, cols, _d = WHERE[name]
        if hi is None:
            hi = cols
        ap = T[buf][:, o + lo:o + hi] if step == 1 else T[buf][:, o + lo:o + hi:step]
        return (ap, [(name, lo, hi, step)], (hi - lo + step - 1) // step, False)

    def IND(w, off):
        return (w[0].indirect(off[0]), w[1] + off[1], 16 * off[2], True)

    def regs(*xs):
        out = []
        for x in xs:
            if isinstance(x, tuple):
                out += x[1]
        return out

    def val(x):
        return x[0] if isinstance(x, tuple) else x

    def kind(x):
        return WHERE[x[1][0][0]][3]

    def half(*xs):
        return 0.5 if all(kind(x) in ("bfloat16", "float16", "uint16") for x in xs) else 1

    def vc(n, gath=False):
        return (0.055, n, gath)

    def tt(out, a, b, op):
        n = out[2] * (1 if a[3] or _bank(a[1][0]) or _bank(b[1][0]) else 2)
        return add("v", lambda e: e.tensor_tensor(out=out[0], in0=a[0], in1=b[0], op=op), regs(a, b), regs(out), vc(n, a[3]))

    def ts(out, a, s1, s2, op0, op1=None):
        if op1 is None:
            fn = lambda e: e.tensor_scalar(out=out[0], in0=a[0], scalar1=val(s1), scalar2=None, op0=op0)
        else:
            fn = lambda e: e.tensor_scalar(out=out[0], in0=a[0], scalar1=val(s1), scalar2=val(s2), op0=op0, op1=op1)
        return add("v", fn, regs(a, s1, s2), regs(out), vc(out[2] * half(out, a)))

    def vcp(out, a):
        return add("v", lambda e: e.tensor_copy(out=out[0], in_=a[0]), regs(a), regs(out),
                   vc(out[2], True) if a[3] else vc(out[2] * half(out, a)))

    def scan(out, d0, d1, op0, op1):
        return add("v", lambda e: e.tensor_tensor_scan(out=out[0], data0=d0[0], data1=d1[0], initial=0.0, op0=op0, op1=op1),
                   regs(d0, d1), regs(out), vc(out[2] * half(out, d0, d1)))

    def vtr(out, a):
        return add("v", lambda e: e.transpose(out=out[0], in_=a[0]), regs(a), regs(out), vc(out[2]))

    def fill(out, x):
        return add("v", lambda e: e.memset(out[0], x), [], regs(out), vc(out[2] * half(out)))

    def act(out, a, func, bias=None):
        if bias is None:
            fn = lambda e: e.activation(out=out[0], in_=a[0], func=func)
        else:
            fn = lambda e: e.activation(out=out[0], in_=a[0], func=func, bias=val(bias))
        return add("s", fn, regs(a, bias), regs(out), (0.065, out[2], a[3]))

    def mm(out, l, r, start, stop):
        return add("t", lambda e: e.matmul(out[0], l[0], r[0], start, stop), regs(l, r), regs(out),
                   (0.03, max(64, r[2]) * (4 if kind(r) == "float32" else 1), False))

    def sel(out, a, pattern, op, base, cm):
        return add("g", lambda e: e.affine_select(out=out[0], in_=a[0], pattern=pattern, compare_op=op, fill=0.0, base=base,
                                                 channel_multiplier=cm), regs(a), regs(out), (0.2, 2 * out[2], False))

    def iota(out, pattern, base, cm):
        if kind(out) != "int32":
            fn = lambda e: e.iota(out[0], pattern=pattern, base=base, channel_multiplier=cm, allow_small_or_imprecise_dtypes=True)
        else:
            fn = lambda e: e.iota(out[0], pattern=pattern, base=base, channel_multiplier=cm)
        return add("g", fn, [], regs(out), (0.15, 2 * out[2], False))

    def load(q, name, out):
        return add(q, lambda e: e.dma_start(out=out[0], in_=T[name][:, :]), [], regs(out), (0.1, 0, False), 2.2,
                   "ld_" + name, 16, True)

    dst = T.cores[(rank - 1) % len(T.cores)]
    src = T.cores[(rank + 1) % len(T.cores)]
    rid, pid = topo.addr(dst, core)
    es = topo.engines(core, dst)[:8]
    mask = sum(1 << e for e in es)
    n_in = len(topo.engines(src, core)[:8])

    def send(slot, a, land):
        j = add("g", lambda e: e.remote_dma(land[0], a[0], T.sem["arr%d" % slot], T.sem.loc, pid, rid, mask),
                regs(a), [], (0.3, 0, False))
        ops[j]["remote"] = True
        add("x", None, [], regs(land), (0.0, 0, False), 2.5, "arr%d" % slot, n_in, True, (j,))

    own0 = A("xw0", XO, XO + V)
    load("y", "snd", A("sndi"))
    load("s", "xa", own0)
    load("y", "ent", A("enti"))
    load("y", "yc", A("xw0", YO, XE))
    load("s", "bn", A("bt"))
    load("y", "usr", A("usri"))
    load("s", "th", A("thi"))
    for c in range(4):
        ts(A("sndu", 6 * c, 6 * c + 6), A("sndi", 6 * c, 6 * c + 6), 4, c, OP.mult, OP.add)
    act(A("gs0"), IND(own0, A("sndu")), AF.Copy)
    send(4, A("gs0"), A("xw0", XG, XG + NG))

    fill(A("one"), 1.0)
    fill(A("one144"), 1.0)
    fill(A("oe"), 1.0)
    sel(A("idn"), A("one"), [[-1, 128]], OP.is_equal, 0, 1)
    sel(A("blkh"), A("one144"), [[-16, 9], [0, 16]], OP.is_ge, 0, 1)
    sel(A("blk"), A("blkh"), [[16, 9], [0, 16]], OP.is_ge, 15, -1)
    sel(A("wsel"), A("blk"), [[0, 9], [1, 16]], OP.is_equal, -15, 0)
    sel(A("ee0"), A("oe"), [[1, 128]], OP.is_ge, 0, -16)
    sel(A("ee"), A("ee0"), [[-1, 128]], OP.is_ge, 15, 16)
    iota(A("ji"), [[1, NBT]], 128, -1)
    iota(A("jc"), [[1, NBT]], 0, 0)
    iota(A("pi"), [[0, 4]], 0, 1)
    iota(A("bi"), [[NBT, 4]], 0, 0)
    for name, of, x in (("half", "idn", 0.5), ("neg", "idn", -1.0), ("i256", "idn", 256.0), ("i1152", "idn", 1152.0),
                        ("idf", "idn", 1.0), ("w32", "wsel", 32.0), ("w16", "wsel", 16.0),
                        ("wn16", "wsel", -16.0)):
        ts(A(name), A(of), x, None, OP.mult)
    for name, x in (("b16", 0.0625), ("b1", 1.0), ("b4096", 4096.0), ("dead", -8192.0), ("blkf", 1.0)):
        ts(A(name), A("blk", 0, 128), x, None, OP.mult)
    ts(A("pj"), A("pi"), 15, None, OP.bitwise_and)
    vcp(A("pf"), A("pj"))
    ts(A("py"), A("pf", 0, 1), -0.0625, None, OP.mult)
    ts(A("bc"), A("pf"), -4096.0, None, OP.mult)
    tt(A("bc"), A("bc"), A("bi"), OP.add)
    ts(A("jj"), A("ji"), 15, None, OP.bitwise_and)
    ts(A("mask"), A("jj"), 0, -4096.0, OP.not_equal, OP.mult)
    ts(A("kc"), A("one", 0, NBT), A("pf", 0, 1), None, OP.mult)
    ts(A("yc96"), A("one", 0, NBT), A("py"), None, OP.mult)
    for name, x, y in (("cm", MAGIC, None), ("cq", -0.25, None), ("rx", 1.0, 0.0), ("rn", 0.0, 512.0), ("rg", 0.0, 1048576.0),
                       ("rm0", 0.0, None), ("rm1", 0.0, None), ("mgc", -MAGIC, None), ("nzc", -float(ZC), None)):
        fill(A(name), x)
        if y is not None:
            fill(A(name, 0, WHERE[name][2], 16), y)
    ts(A("entt"), A("enti"), float(ZC), None, OP.add)
    ts(A("ct"), A("enti"), 1152.0, 1024.0, OP.is_ge, OP.mult)
    ts(A("uw"), A("usri"), 4, None, OP.logical_shift_right)
    ts(A("uq"), A("usri"), 15, None, OP.bitwise_and)
    vcp(A("thf"), A("thi"))
    mm(A("p0", 0, 5), A("ee"), A("thf"), True, True)
    vcp(A("tha"), A("p0", 0, 5))
    vcp(A("thc", 0, 1), A("tha", 0, 1))
    act(A("xw1", XO, XO + V), own0, AF.Copy)
    act(A("xw1", YO, XE), A("xw0", YO, XE), AF.Copy)
    act(A("xw1", XG, XG + NG), A("xw0", XG, XG + NG), AF.Copy)

    I = A("idn")
    RXL = A("rx", 0, NBT)

    def sl(b, t, base=0):
        return base + 384 * b + t % 4, base + 384 * (b + 1), 4

    def xcopy(b, t):
        for m in range(4):
            mm(A("p%d" % (4 + b), m, 384, 4), I, A("xw%d" % b, *sl(b, t, XO)), True, True)

    def scans(G, X, N, parts):
        w = 16 * NBT // parts
        for m in range(parts):
            lo, hi = w * m, w * m + w
            scan(A(X, lo, hi), A("rx", lo, hi), A(G, lo, hi), OP.mult, OP.max)
            scan(A(N, lo, hi), A("rn", lo, hi), A(G, lo, hi), OP.add, OP.min)

    def gather(out, win, off, vec=()):
        w = NBT // PARTS
        for m in range(PARTS):
            o, i = A(out, 16 * w * m, 16 * w * m + 16 * w), IND(win, A(off, w * m, w * m + w))
            if m in vec:
                vcp(o, i)
            else:
                act(o, i, AF.Copy)

    def fin(bank, bv, X, N, out):
        p = A(bank, 0, NBT)
        mm(p, I, A("cq"), True, False)
        mm(p, A("neg"), bv, False, False)
        mm(p, A("half"), A(X, 15, 16 * NBT, 16), False, False)
        mm(p, A("half"), A(N, 15, 16 * NBT, 16), False, False)
        mm(p, I, A("cm"), False, True)
        act(out, p, AF.Abs, A("mgc"))

    for b in range(2):
        xcopy(b, 0)
    for t in range(5):
        last = t == 4
        start[:] = [len(ops)]
        for b in range(2):
            s = str(b)
            vcp(A("eu" + s), A("entt", *sl(b, t)))
            gather("ga" + s, A("xw" + s), "eu" + s, (1,) if b == 0 else ())
        if last:
            act(A("yef"), A("entt"), AF.Identity, A("nzc"))
            start[0] += 1
        for b in range(2):
            s = str(b)
            b0, b1 = "p%d" % (2 * b), "p%d" % (2 * b + 1)
            xb, fb = "p%d" % (4 + b), "p%d" % (6 + b)
            K = A(b0, 0, NBT)
            mm(K, A("i256"), A("ct", *sl(b, t)), True, False)
            mm(K, I, A("kc"), False, False)
            for k in range(4):
                tt(A("mt" + s, 384 * k, 384 * k + 384), A(xb, 0, 384), A("ga" + s, k, 1536, 4), OP.subtract if b else OP.max)
            if b:
                for lo in range(0, 16 * NBT, 4 * NBT):
                    act(A("ab1", lo, lo + 4 * NBT), A("mt1", lo, lo + 4 * NBT), AF.Abs)
            else:
                for k in range(16):
                    mm(K, A("wn16", 15 - k, 143 - k), A("ga0", k, 1536, 16), False, False)
            for k in sorted(range(16), key=lambda k: k % 4):
                lo = 384 * (k % 4)
                mm(K, A("w16" if b else "w32", 15 - k, 143 - k), A("ab1" if b else "mt0", lo + k // 4, lo + 384, 4), False, k == 15)
            vtr(A("kt" + s), K)
            scan(A("r1" + s), A("rg"), A("kt" + s), OP.add, OP.min)
            ts(A("rm" + s, 15, NBT, 16), A("r1" + s, 15, NBT, 16), 262143.0, None, OP.min)
            scan(A("mb" + s), RXL, A("rm" + s, 15, 15 + NBT), OP.mult, OP.add)
            vtr(A("mbt" + s), A("mb" + s))
            tt(A("hit" + s), K, A("mbt" + s), OP.is_equal)
            E = A(b1, 0, NBT)
            mm(E, A("idf"), A("entt", *sl(b, t)), True, False)
            mm(E, A("i1152"), A("hit" + s), False, True)
            vcp(A("ou" + s), E)
            gather("gb" + s, A("xw" + s), "ou" + s)
            scans("ga" + s, "m0" + s, "n0" + s, 1)
            fin(fb, A("bt", *sl(b, t)), "m0" + s, "n0" + s, A("f0" + s))
            scans("gb" + s, "mx" + s, "mn" + s, PARTS)
            z = A("xw" + s, 0, NBT)
            fin(b0, A("bt", *sl(b, t)), "mx" + s, "mn" + s, z)
            dz = A(fb, NBT, 2 * NBT)
            mm(dz, A("neg"), A("f0" + s), True, False)
            mm(dz, I, z, False, True)
        if not last:
            for b in range(2):
                xcopy(b, t + 1)
        else:
            start[0] -= 8
        for h in range(1, 4):
            for b in range(2):
                s = str(b)
                b0, b1 = "p%d" % (2 * b), "p%d" % (2 * b + 1)
                z = A("xw" + s, NBT * (h - 1), NBT * h)
                wl = A("wl" + s, 0, 6)
                Y = A(b1, 0, NBT)
                mm(Y, I, A("yc96"), True, False)
                mm(Y, A("b16"), z, False, True)
                R = A(b1, NBT, 2 * NBT)
                mm(R, I, A("yc96"), True, False)
                mm(R, A("b16"), z, False, False)
                mm(R, I, A("cm"), False, True)
                act(A("ri" + s), R, AF.Identity, A("mgc"))
                tt(A("hot" + s), Y, A("ri" + s), OP.is_equal)
                for tab, out in (("uw", "pw"), ("uq", "pq")):
                    tt(A(out + s), A(tab, *sl(b, t)) if h == 1 else IND(A(tab), wl), A("hot" + s), OP.mult)
                W = A(b0, 0, NBT)
                mm(W, I, A("mask"), True, False)
                mm(W, A("blkf"), A("pw" + s), False, True)
                Q = A(b1, 0, NBT)
                mm(Q, I, A("jc"), True, False)
                mm(Q, A("b4096"), A("pq" + s), False, True)
                act(A("aa" + s), Q, AF.Abs, A("bc", h - 1, h))
                scan(A("ll" + s), RXL, W, OP.mult, OP.max)
                vcp(wl, A("ll" + s, 15, NBT, 16))
                tt(A("of" + s), IND(A("entt"), wl), A("aa" + s), OP.min)
                vcp(A("ou" + s), A("of" + s))
                tt(A("da%d%s" % (h, s)), IND(A("ct"), wl), A("aa" + s), OP.is_gt)
                act(A("bw" + s), IND(A("bt"), wl), AF.Copy)
                gather("gb" + s, A("xw" + s), "ou" + s)
                if h == 3:
                    act(A("xv" + s), IND(A("xw" + s, XO, XO + V), wl), AF.Copy)
                scans("gb" + s, "mx" + s, "mn" + s, PARTS)
                fin(b0, A("bw" + s), "mx" + s, "mn" + s,
                    A("xw" + s, NBT * h, NBT * (h + 1)) if h < 3 else A("z3" + s))
        for b in range(2):
            s = str(b)
            b0, b1, fb = "p%d" % (2 * b), "p%d" % (2 * b + 1), "p%d" % (6 + b)
            d = A(b1, 0, NBT)
            mm(d, A("neg"), A("xv" + s), True, False)
            mm(d, I, A("z3" + s), False, True)
            act(A("da" + s), d, AF.Abs)
            D = A(b0, 0, NBT)
            for h in range(1, 4):
                mm(D, A("dead"), A("da%d%s" % (h, s)), h == 1, False)
            mm(D, A("b1"), A("da" + s), False, True)
            ts(A("st" + s), D, A("thc", t, t + 1), None, OP.is_le)
            tt(A("sd" + s), A(fb, NBT, 2 * NBT), A("st" + s), OP.mult)
            xn = A(b1, 0, NBT)
            mm(xn, I, A("f0" + s), True, False)
            mm(xn, I, A("sd" + s), False, True)
        for b in range(2):
            xn = A("p%d" % (2 * b + 1), 0, NBT)
            if b == 0:
                act(A("xw0", *sl(b, t, XO)), xn, AF.Copy)
            else:
                vcp(A("xw0", *sl(b, t, XO)), xn)
        if not last:
            vcp(A("gt%d" % t), IND(own0, A("sndu", 6 * t, 6 * t + 6)))
            send(t, A("gt%d" % t), A("land%d" % t))
        for b in range(2):
            s = str(b)
            b0, b1 = "p%d" % (2 * b), "p%d" % (2 * b + 1)
            tt(A("hs" + s), A("st" + s), A("hit" + s), OP.mult)
            E = A(b0, 0, NBT)
            mm(E, A("idf"), A("entt", *sl(b, t)), True, False)
            mm(E, A("i1152"), A("hs" + s), False, True)
            if last:
                act(A("yef", *sl(b, t)), E, AF.Identity, A("nzc"))
                cols = slice(384 * b, 384 * b + 384)
                xc = slice(XO + 384 * b, XO + 384 * b + 384)
                add("y", lambda e, cols=cols: e.dma_start(out=T.ye[:, cols], in_=T.yef[:, cols]),
                    [("yef", cols.start, cols.stop, 1)], [], (0.1, 0, False), 2.0, "o%d" % b, 16, True)
                add("y", lambda e, cols=cols, xc=xc: e.dma_start(out=T.yx[:, cols], in_=T.xw0[:, xc]),
                    [("xw0", xc.start, xc.stop, 1)], [], (0.1, 0, False), 2.0, "o%d" % (2 + b), 16, True)
            else:
                act(A("entt", *sl(b, t)), E, AF.Copy)
                ts(A("ct", *sl(b, t)), A("entt", *sl(b, t)), 1440.0, 1024.0, OP.is_ge, OP.mult)
                act(A("xw1", *sl(b, t, XO)), A("p%d" % (2 * b + 1), 0, NBT), AF.Copy)
        if not last:
            C = A("p0", 0, NBT)
            mm(C, A("one"), A("hs0"), True, False)
            mm(C, A("one"), A("hs1"), False, True)
            rr, c0 = A("rr"), A("p0", 0, NBT)
            add("v", lambda e, rr=rr, c0=c0: e.tensor_reduce(out=rr[0], in_=c0[0], axis=AX.X, op=OP.add),
                regs(c0), regs(rr), vc(NBT))
            vcp(A("rri"), A("rr"))
            ts(A("rrj"), A("rri"), 31, None, OP.bitwise_and)
            tt(A("thc", t + 1, t + 2), A("rrj"), A("tha", t + 1, t + 2), OP.add)
            for b in range(2):
                vcp(A("xw%d" % b, XG + NBT * t, XG + NBT * (t + 1)), A("land%d" % t))

    _edges(ops)
    if "order" not in PLAN:
        PLAN["order"] = _plan(ops)
    needed = [False] * len(ops)
    for o in ops:
        for j in o["pre"]:
            needed[j] = needed[j] or o["pre"][j]
    know = {}
    count = {}
    remotes = 0
    for i in PLAN["order"]:
        o = ops[i]
        q = o["q"]
        if q == "x":
            count[o["sem"]] = o["amount"]
            o["done"] = (o["sem"], o["amount"])
            o["snap"] = {}
            continue
        kq = know.setdefault(q, {})
        want = sorted((j for j in o["pre"] if o["pre"][j]), key=lambda j: -j)
        for j in want:
            sm, c = ops[j]["done"]
            if kq.get(sm, 0) < c:
                same = [j2 for j2 in want if ops[j2]["done"][0] == sm]
                c = max(ops[j2]["done"][1] for j2 in same)
                eng[q].wait_ge(T.sem[sm], c)
                kq[sm] = c
                for j2 in same:
                    for a in ops[j2]["snap"]:
                        kq[a] = max(kq.get(a, 0), ops[j2]["snap"][a])
        ins = o["fn"](eng[q])
        o["snap"] = dict(kq)
        if o["remote"]:
            remotes += 1
            continue
        if o["sem"] or needed[i]:
            sm = o["sem"] or QS[q]
            count[sm] = count.get(sm, 0) + o["amount"]
            ins.then_inc(T.sem[sm], o["amount"])
            o["done"] = (sm, count[sm])
            if not o["sem"]:
                o["snap"][sm] = count[sm]
    for sm in sorted(count):
        g.wait_ge(T.sem[sm], count[sm])
    g.wait_ge(T.sem.loc, remotes * len(es))
